import numpy as np
import ml_dtypes

BF16 = ml_dtypes.bfloat16


def bf(x):
    return np.asarray(x, np.float32).astype(BF16)


def f32(x):
    return np.asarray(x, np.float32)


def f64(x):
    return np.asarray(x).astype(np.float64)


def striped(idx):
    return np.tile(idx.reshape(-1, 16).T, (8, 1))


def rows(idx, k):
    return np.tile(idx, (k, 1))


def look(tab, idx):
    return np.take_along_axis(f64(tab), rows(idx, len(tab)), axis=1)


K, S, V, N = 256, 2048, 512, 512


def setup_inputs():
    return {"tab": f32(np.random.standard_normal((2, K, S))), "y": f32(np.random.standard_normal((K, V))), "offs": striped(np.random.permutation(S)[:N])}


def reference(tab, y, offs):
    idx = offs[:16].T.reshape(-1)
    x = (np.maximum(look(tab[0], idx), f64(y))) * (np.maximum(look(tab[1], idx), 0.0))
    return x

@@ -1,0 +1,57 @@
+import concourse.mybir as mybir
+
+F32, U16 = mybir.dt.float32, mybir.dt.uint16
+MAX, MULT = mybir.AluOpType.max, mybir.AluOpType.mult
+RELU = mybir.ActivationFunctionType.Relu
+
+P = 128
+ROWS = 256
+PLACES = 2048
+N = 512
+BLOCKS = ROWS // P
+PIECES = 4
+PIECE = N // PIECES
+COLS = PIECE // 16
+
+FLOPS = 3 * ROWS * N
+
+
+def tile_lookup_vg_maxrelu_out_kernel(tc, tab, y, offs, out):
+    nc = tc.nc
+    with (
+        tc.tile_pool(name="held", bufs=1) as held,
+        tc.tile_pool(name="blocks", bufs=BLOCKS) as blocks,
+    ):
+        offsets = held.tile([P, N // 16], U16, name="offsets")
+        nc.sync.dma_start(offsets[:], offs)
+
+        zeros = held.tile([P, 1], F32, name="zeros")
+        warmed = held.tile([P, 1], F32, name="warmed")
+        nc.vector.memset(zeros[:], 0.0)
+        nc.scalar.activation(warmed[:], zeros[:], RELU)
+
+        tops = []
+        for b in range(BLOCKS):
+            rows = slice(b * P, (b + 1) * P)
+            stream = blocks.tile([P, N], F32, name="stream")
+            nc.sync.dma_start(stream[:], y[rows, :])
+            values = blocks.tile([P, PLACES], F32, name="values")
+            nc.sync.dma_start(values[:], tab[0, rows, :])
+            top = blocks.tile([P, N], F32, name="top")
+            nc.vector.tensor_tensor(top[:], values[:].indirect(offsets[:]), stream[:], MAX)
+            tops.append(top)
+
+        for b in range(BLOCKS):
+            rows = slice(b * P, (b + 1) * P)
+            gates = blocks.tile([P, PLACES], F32, name="gates")
+            nc.sync.dma_start(gates[:], tab[1, rows, :])
+            gate = blocks.tile([P, N], F32, name="gate")
+            top = tops[b]
+            product = blocks.tile([P, N], F32, name="product")
+            for k in range(PIECES):
+                piece = slice(k * PIECE, (k + 1) * PIECE)
+                nc.scalar.activation(
+                    gate[:, piece], gates[:].indirect(offsets[:, k * COLS : (k + 1) * COLS]), RELU
+                )
+                nc.vector.tensor_tensor(product[:, piece], top[:, piece], gate[:, piece], MULT)
+                nc.sync.dma_start(out[rows, piece], product[:, piece])

@@ -18,40 +18,35 @@ FLOPS = 3 * ROWS * N
 
 def tile_lookup_vg_maxrelu_out_kernel(tc, tab, y, offs, out):
     nc = tc.nc
-    with (
-        tc.tile_pool(name="held", bufs=1) as held,
-        tc.tile_pool(name="blocks", bufs=BLOCKS) as blocks,
-    ):
+    value_rows = tab[0].rearrange("(p b) s -> b p s", b=BLOCKS)
+    gate_rows = tab[1].rearrange("(p b) s -> b p s", b=BLOCKS)
+    out_rows = out.rearrange("(p b) j -> b p j", b=BLOCKS)
+    with tc.tile_pool(name="held", bufs=1) as held:
         offsets = held.tile([P, N // 16], U16, name="offsets")
+        stream = held.tile([P, BLOCKS, N], F32, name="stream")
+        values = [held.tile([P, PLACES], F32, name=f"values{b}") for b in range(BLOCKS)]
+        gates = [held.tile([P, PLACES], F32, name=f"gates{b}") for b in range(BLOCKS)]
+        top = [held.tile([P, N], F32, name=f"top{b}") for b in range(BLOCKS)]
+        gate = [held.tile([P, N], F32, name=f"gate{b}") for b in range(BLOCKS)]
+        product = [held.tile([P, N], F32, name=f"product{b}") for b in range(BLOCKS)]
+
+        nc.sync.dma_start(gates[0][:], gate_rows[0])
         nc.sync.dma_start(offsets[:], offs)
-
-        zeros = held.tile([P, 1], F32, name="zeros")
-        warmed = held.tile([P, 1], F32, name="warmed")
-        nc.vector.memset(zeros[:], 0.0)
-        nc.scalar.activation(warmed[:], zeros[:], RELU)
-
-        tops = []
+        nc.sync.dma_start(stream[:], y.rearrange("(p b) j -> p b j", b=BLOCKS))
         for b in range(BLOCKS):
-            rows = slice(b * P, (b + 1) * P)
-            stream = blocks.tile([P, N], F32, name="stream")
-            nc.sync.dma_start(stream[:], y[rows, :])
-            values = blocks.tile([P, PLACES], F32, name="values")
-            nc.sync.dma_start(values[:], tab[0, rows, :])
-            top = blocks.tile([P, N], F32, name="top")
-            nc.vector.tensor_tensor(top[:], values[:].indirect(offsets[:]), stream[:], MAX)
-            tops.append(top)
+            nc.sync.dma_start(values[b][:], value_rows[b])
+        nc.sync.dma_start(gates[1][:], gate_rows[1])
 
-        for b in range(BLOCKS):
-            rows = slice(b * P, (b + 1) * P)
-            gates = blocks.tile([P, PLACES], F32, name="gates")
-            nc.sync.dma_start(gates[:], tab[1, rows, :])
-            gate = blocks.tile([P, N], F32, name="gate")
-            top = tops[b]
-            product = blocks.tile([P, N], F32, name="product")
-            for k in range(PIECES):
-                piece = slice(k * PIECE, (k + 1) * PIECE)
-                nc.scalar.activation(
-                    gate[:, piece], gates[:].indirect(offsets[:, k * COLS : (k + 1) * COLS]), RELU
-                )
-                nc.vector.tensor_tensor(product[:, piece], top[:, piece], gate[:, piece], MULT)
-                nc.sync.dma_start(out[rows, piece], product[:, piece])
+        nc.scalar.activation(gate[0][:], gates[0][:].indirect(offsets[:]), RELU)
+        nc.vector.tensor_tensor(top[0][:], values[0][:].indirect(offsets[:]), stream[:, 0, :], MAX)
+        nc.vector.tensor_tensor(product[0][:], top[0][:], gate[0][:], MULT)
+        nc.sync.dma_start(out_rows[0], product[0][:])
+
+        nc.vector.tensor_tensor(top[1][:], values[1][:].indirect(offsets[:]), stream[:, 1, :], MAX)
+        for k in range(PIECES):
+            piece = slice(k * PIECE, (k + 1) * PIECE)
+            nc.scalar.activation(
+                gate[1][:, piece], gates[1][:].indirect(offsets[:, k * COLS : (k + 1) * COLS]), RELU
+            )
+            nc.vector.tensor_tensor(product[1][:, piece], top[1][:, piece], gate[1][:, piece], MULT)
+            nc.sync.dma_start(out_rows[1][:, piece], product[1][:, piece])

@@ -9,9 +9,10 @@ ROWS = 256
 PLACES = 2048
 N = 512
 BLOCKS = ROWS // P
-PIECES = 4
-PIECE = N // PIECES
-COLS = PIECE // 16
+STRIPE = 16
+PIECE = 128
+LATE = PIECE
+EARLY = BLOCKS * N - LATE
 
 FLOPS = 3 * ROWS * N
 
@@ -20,33 +21,44 @@ def tile_lookup_vg_maxrelu_out_kernel(tc, tab, y, offs, out):
     nc = tc.nc
     value_rows = tab[0].rearrange("(p b) s -> b p s", b=BLOCKS)
     gate_rows = tab[1].rearrange("(p b) s -> b p s", b=BLOCKS)
+    y_pairs = y.rearrange("(p b) j -> p (b j)", b=BLOCKS)
     out_rows = out.rearrange("(p b) j -> b p j", b=BLOCKS)
     with tc.tile_pool(name="held", bufs=1) as held:
-        offsets = held.tile([P, N // 16], U16, name="offsets")
-        stream = held.tile([P, BLOCKS, N], F32, name="stream")
+        offsets = held.tile([P, N // STRIPE], U16, name="offsets")
+        stream = held.tile([P, BLOCKS * N], F32, name="stream")
         values = [held.tile([P, PLACES], F32, name=f"values{b}") for b in range(BLOCKS)]
         gates = [held.tile([P, PLACES], F32, name=f"gates{b}") for b in range(BLOCKS)]
         top = [held.tile([P, N], F32, name=f"top{b}") for b in range(BLOCKS)]
         gate = [held.tile([P, N], F32, name=f"gate{b}") for b in range(BLOCKS)]
         product = [held.tile([P, N], F32, name=f"product{b}") for b in range(BLOCKS)]
 
-        nc.sync.dma_start(gates[0][:], gate_rows[0])
+        def entries(first, last):
+            return offsets[:, first // STRIPE : last // STRIPE]
+
+        def look_up_values(b, first, last):
+            picked = values[b][:].indirect(entries(first, last))
+            nc.vector.tensor_tensor(top[b][:, first:last], picked, stream[:, b * N + first : b * N + last], MAX)
+
+        def gate_and_store(b, first, last):
+            nc.scalar.activation(gate[b][:, first:last], gates[b][:].indirect(entries(first, last)), RELU)
+            nc.vector.tensor_tensor(product[b][:, first:last], top[b][:, first:last], gate[b][:, first:last], MULT)
+            nc.sync.dma_start(out_rows[b][:, first:last], product[b][:, first:last])
+
+        nc.scalar.dma_start(stream[:, :EARLY], y_pairs[:, :EARLY])
         nc.sync.dma_start(offsets[:], offs)
-        nc.sync.dma_start(stream[:], y.rearrange("(p b) j -> p b j", b=BLOCKS))
+        nc.sync.dma_start(gates[0][:], gate_rows[0])
         for b in range(BLOCKS):
             nc.sync.dma_start(values[b][:], value_rows[b])
         nc.sync.dma_start(gates[1][:], gate_rows[1])
+        nc.sync.dma_start(stream[:, EARLY:], y_pairs[:, EARLY:])
 
-        nc.scalar.activation(gate[0][:], gates[0][:].indirect(offsets[:]), RELU)
-        nc.vector.tensor_tensor(top[0][:], values[0][:].indirect(offsets[:]), stream[:, 0, :], MAX)
-        nc.vector.tensor_tensor(product[0][:], top[0][:], gate[0][:], MULT)
-        nc.sync.dma_start(out_rows[0], product[0][:])
+        look_up_values(0, 0, N)
+        for first in range(0, N, PIECE):
+            gate_and_store(0, first, first + PIECE)
 
-        nc.vector.tensor_tensor(top[1][:], values[1][:].indirect(offsets[:]), stream[:, 1, :], MAX)
-        for k in range(PIECES):
-            piece = slice(k * PIECE, (k + 1) * PIECE)
-            nc.scalar.activation(
-                gate[1][:, piece], gates[1][:].indirect(offsets[:, k * COLS : (k + 1) * COLS]), RELU
-            )
-            nc.vector.tensor_tensor(product[1][:, piece], top[1][:, piece], gate[1][:, piece], MULT)
-            nc.sync.dma_start(out_rows[1][:, piece], product[1][:, piece])
+        look_up_values(1, 0, N - LATE)
+        look_up_values(1, N - LATE, N)
+        for first in range(0, N - PIECE, PIECE):
+            gate_and_store(1, first, first + PIECE)
+        for first in range(N - PIECE, N, PIECE // 2):
+            gate_and_store(1, first, first + PIECE // 2)

@@ -23,42 +23,42 @@ def tile_lookup_vg_maxrelu_out_kernel(tc, tab, y, offs, out):
     gate_rows = tab[1].rearrange("(p b) s -> b p s", b=BLOCKS)
     y_pairs = y.rearrange("(p b) j -> p (b j)", b=BLOCKS)
     out_rows = out.rearrange("(p b) j -> b p j", b=BLOCKS)
-    with tc.tile_pool(name="held", bufs=1) as held:
+    with tc.tile_pool(name="held", bufs=1) as held, tc.tile_pool(name="reused", bufs=1) as reused:
         offsets = held.tile([P, N // STRIPE], U16, name="offsets")
-        stream = held.tile([P, BLOCKS * N], F32, name="stream")
+        early = held.tile([P, EARLY], F32, name="early")
         values = [held.tile([P, PLACES], F32, name=f"values{b}") for b in range(BLOCKS)]
         gates = [held.tile([P, PLACES], F32, name=f"gates{b}") for b in range(BLOCKS)]
         top = [held.tile([P, N], F32, name=f"top{b}") for b in range(BLOCKS)]
         gate = [held.tile([P, N], F32, name=f"gate{b}") for b in range(BLOCKS)]
-        product = [held.tile([P, N], F32, name=f"product{b}") for b in range(BLOCKS)]
 
         def entries(first, last):
             return offsets[:, first // STRIPE : last // STRIPE]
 
-        def look_up_values(b, first, last):
+        def look_up_values(b, first, last, stream):
             picked = values[b][:].indirect(entries(first, last))
-            nc.vector.tensor_tensor(top[b][:, first:last], picked, stream[:, b * N + first : b * N + last], MAX)
+            nc.vector.tensor_tensor(top[b][:, first:last], picked, stream, MAX)
 
-        def gate_and_store(b, first, last):
+        def gate_and_store(b, first, last, product):
             nc.scalar.activation(gate[b][:, first:last], gates[b][:].indirect(entries(first, last)), RELU)
-            nc.vector.tensor_tensor(product[b][:, first:last], top[b][:, first:last], gate[b][:, first:last], MULT)
-            nc.sync.dma_start(out_rows[b][:, first:last], product[b][:, first:last])
+            nc.vector.tensor_tensor(product[:, first:last], top[b][:, first:last], gate[b][:, first:last], MULT)
+            nc.sync.dma_start(out_rows[b][:, first:last], product[:, first:last])
 
-        nc.scalar.dma_start(stream[:, :EARLY], y_pairs[:, :EARLY])
-        nc.sync.dma_start(offsets[:], offs)
+        late = reused.tile([P, LATE], F32, name="late", tag="late_then_product")
+        nc.scalar.dma_start(early[:], y_pairs[:, :EARLY])
         nc.sync.dma_start(gates[0][:], gate_rows[0])
+        nc.sync.dma_start(offsets[:], offs)
         for b in range(BLOCKS):
             nc.sync.dma_start(values[b][:], value_rows[b])
         nc.sync.dma_start(gates[1][:], gate_rows[1])
-        nc.sync.dma_start(stream[:, EARLY:], y_pairs[:, EARLY:])
+        nc.sync.dma_start(late[:], y_pairs[:, EARLY:])
 
-        look_up_values(0, 0, N)
+        look_up_values(0, 0, N, early[:, :N])
+        product = held.tile([P, N], F32, name="product")
         for first in range(0, N, PIECE):
-            gate_and_store(0, first, first + PIECE)
+            gate_and_store(0, first, first + PIECE, product)
 
-        look_up_values(1, 0, N - LATE)
-        look_up_values(1, N - LATE, N)
-        for first in range(0, N - PIECE, PIECE):
-            gate_and_store(1, first, first + PIECE)
-        for first in range(N - PIECE, N, PIECE // 2):
-            gate_and_store(1, first, first + PIECE // 2)
+        look_up_values(1, 0, N - LATE, early[:, N:])
+        look_up_values(1, N - LATE, N, late[:])
+        last_product = reused.tile([P, N], F32, name="last_product", tag="late_then_product")
+        for first in range(0, N, PIECE):
+            gate_and_store(1, first, first + PIECE, last_product)

@@ -11,7 +11,7 @@ N = 512
 BLOCKS = ROWS // P
 STRIPE = 16
 PIECE = 128
-LATE = PIECE
+LATE = PIECE // 2
 EARLY = BLOCKS * N - LATE
 
 FLOPS = 3 * ROWS * N

@@ -11,7 +11,8 @@ N = 512
 BLOCKS = ROWS // P
 STRIPE = 16
 PIECE = 128
-LATE = PIECE // 2
+SHORT = PIECE // 2
+LATE = SHORT + PIECE
 EARLY = BLOCKS * N - LATE
 
 FLOPS = 3 * ROWS * N
@@ -23,7 +24,7 @@ def tile_lookup_vg_maxrelu_out_kernel(tc, tab, y, offs, out):
     gate_rows = tab[1].rearrange("(p b) s -> b p s", b=BLOCKS)
     y_pairs = y.rearrange("(p b) j -> p (b j)", b=BLOCKS)
     out_rows = out.rearrange("(p b) j -> b p j", b=BLOCKS)
-    with tc.tile_pool(name="held", bufs=1) as held, tc.tile_pool(name="reused", bufs=1) as reused:
+    with tc.tile_pool(name="held", bufs=1) as held:
         offsets = held.tile([P, N // STRIPE], U16, name="offsets")
         early = held.tile([P, EARLY], F32, name="early")
         values = [held.tile([P, PLACES], F32, name=f"values{b}") for b in range(BLOCKS)]
@@ -43,14 +44,15 @@ def tile_lookup_vg_maxrelu_out_kernel(tc, tab, y, offs, out):
             nc.vector.tensor_tensor(product[:, first:last], top[b][:, first:last], gate[b][:, first:last], MULT)
             nc.sync.dma_start(out_rows[b][:, first:last], product[:, first:last])
 
-        late = reused.tile([P, LATE], F32, name="late", tag="late_then_product")
+        last_product = held.tile([P, N], F32, name="last_product")
+        late = last_product[:, PIECE - SHORT : 2 * PIECE]
         nc.scalar.dma_start(early[:], y_pairs[:, :EARLY])
         nc.sync.dma_start(gates[0][:], gate_rows[0])
         nc.sync.dma_start(offsets[:], offs)
         for b in range(BLOCKS):
             nc.sync.dma_start(values[b][:], value_rows[b])
         nc.sync.dma_start(gates[1][:], gate_rows[1])
-        nc.sync.dma_start(late[:], y_pairs[:, EARLY:])
+        nc.sync.dma_start(late, y_pairs[:, EARLY:])
 
         look_up_values(0, 0, N, early[:, :N])
         product = held.tile([P, N], F32, name="product")
@@ -58,7 +60,7 @@ def tile_lookup_vg_maxrelu_out_kernel(tc, tab, y, offs, out):
             gate_and_store(0, first, first + PIECE, product)
 
         look_up_values(1, 0, N - LATE, early[:, N:])
-        look_up_values(1, N - LATE, N, late[:])
-        last_product = reused.tile([P, N], F32, name="last_product", tag="late_then_product")
-        for first in range(0, N, PIECE):
-            gate_and_store(1, first, first + PIECE, last_product)
+        look_up_values(1, N - LATE, N - PIECE, late[:, :SHORT])
+        look_up_values(1, N - PIECE, N, late[:, SHORT:])
+        for piece in (0, 2, 1, 3):
+            gate_and_store(1, piece * PIECE, (piece + 1) * PIECE, last_product)

@@ -49,17 +49,17 @@ def tile_lookup_vg_maxrelu_out_kernel(tc, tab, y, offs, out):
         nc.scalar.dma_start(early[:], y_pairs[:, :EARLY])
         nc.sync.dma_start(gates[0][:], gate_rows[0])
         nc.sync.dma_start(offsets[:], offs)
-        for b in range(BLOCKS):
+        for b in reversed(range(BLOCKS)):
             nc.sync.dma_start(values[b][:], value_rows[b])
         nc.sync.dma_start(gates[1][:], gate_rows[1])
         nc.sync.dma_start(late, y_pairs[:, EARLY:])
 
+        look_up_values(1, 0, N - LATE, early[:, N:])
         look_up_values(0, 0, N, early[:, :N])
         product = held.tile([P, N], F32, name="product")
         for first in range(0, N, PIECE):
             gate_and_store(0, first, first + PIECE, product)
 
-        look_up_values(1, 0, N - LATE, early[:, N:])
         look_up_values(1, N - LATE, N - PIECE, late[:, :SHORT])
         look_up_values(1, N - PIECE, N, late[:, SHORT:])
         for piece in (0, 2, 1, 3):

@@ -13,6 +13,7 @@ STRIPE = 16
 PIECE = 128
 SHORT = PIECE // 2
 LATE = SHORT + PIECE
+ALIGN = 256
 EARLY = BLOCKS * N - LATE
 
 FLOPS = 3 * ROWS * N
@@ -26,11 +27,11 @@ def tile_lookup_vg_maxrelu_out_kernel(tc, tab, y, offs, out):
     out_rows = out.rearrange("(p b) j -> b p j", b=BLOCKS)
     with tc.tile_pool(name="held", bufs=1) as held:
         offsets = held.tile([P, N // STRIPE], U16, name="offsets")
-        early = held.tile([P, EARLY], F32, name="early")
-        values = [held.tile([P, PLACES], F32, name=f"values{b}") for b in range(BLOCKS)]
-        gates = [held.tile([P, PLACES], F32, name=f"gates{b}") for b in range(BLOCKS)]
-        top = [held.tile([P, N], F32, name=f"top{b}") for b in range(BLOCKS)]
-        gate = [held.tile([P, N], F32, name=f"gate{b}") for b in range(BLOCKS)]
+        early = held.tile([P, EARLY], F32, name="early", align_bytes=ALIGN)
+        values = [held.tile([P, PLACES], F32, name=f"values{b}", align_bytes=ALIGN) for b in range(BLOCKS)]
+        gates = [held.tile([P, PLACES], F32, name=f"gates{b}", align_bytes=ALIGN) for b in range(BLOCKS)]
+        top = [held.tile([P, N], F32, name=f"top{b}", align_bytes=ALIGN) for b in range(BLOCKS)]
+        gate = [held.tile([P, N], F32, name=f"gate{b}", align_bytes=ALIGN) for b in range(BLOCKS)]
 
         def entries(first, last):
             return offsets[:, first // STRIPE : last // STRIPE]
@@ -44,7 +45,7 @@ def tile_lookup_vg_maxrelu_out_kernel(tc, tab, y, offs, out):
             nc.vector.tensor_tensor(product[:, first:last], top[b][:, first:last], gate[b][:, first:last], MULT)
             nc.sync.dma_start(out_rows[b][:, first:last], product[:, first:last])
 
-        last_product = held.tile([P, N], F32, name="last_product")
+        last_product = held.tile([P, N], F32, name="last_product", align_bytes=ALIGN)
         late = last_product[:, PIECE - SHORT : 2 * PIECE]
         nc.scalar.dma_start(early[:], y_pairs[:, :EARLY])
         nc.sync.dma_start(gates[0][:], gate_rows[0])
@@ -56,7 +57,7 @@ def tile_lookup_vg_maxrelu_out_kernel(tc, tab, y, offs, out):
 
         look_up_values(1, 0, N - LATE, early[:, N:])
         look_up_values(0, 0, N, early[:, :N])
-        product = held.tile([P, N], F32, name="product")
+        product = held.tile([P, N], F32, name="product", align_bytes=ALIGN)
         for first in range(0, N, PIECE):
             gate_and_store(0, first, first + PIECE, product)
 

@@ -13,7 +13,7 @@ STRIPE = 16
 PIECE = 128
 SHORT = PIECE // 2
 LATE = SHORT + PIECE
-ALIGN = 256
+ALIGN = 4096
 EARLY = BLOCKS * N - LATE
 
 FLOPS = 3 * ROWS * N
@@ -26,7 +26,7 @@ def tile_lookup_vg_maxrelu_out_kernel(tc, tab, y, offs, out):
     y_pairs = y.rearrange("(p b) j -> p (b j)", b=BLOCKS)
     out_rows = out.rearrange("(p b) j -> b p j", b=BLOCKS)
     with tc.tile_pool(name="held", bufs=1) as held:
-        offsets = held.tile([P, N // STRIPE], U16, name="offsets")
+        offsets = held.tile([P, N // STRIPE], U16, name="offsets", align_bytes=ALIGN)
         early = held.tile([P, EARLY], F32, name="early", align_bytes=ALIGN)
         values = [held.tile([P, PLACES], F32, name=f"values{b}", align_bytes=ALIGN) for b in range(BLOCKS)]
         gates = [held.tile([P, PLACES], F32, name=f"gates{b}", align_bytes=ALIGN) for b in range(BLOCKS)]

@@ -13,7 +13,8 @@ STRIPE = 16
 PIECE = 128
 SHORT = PIECE // 2
 LATE = SHORT + PIECE
-ALIGN = 4096
+ALIGN = 256
+CUTS = [0, *range(PIECE + SHORT, N, PIECE), N]
 EARLY = BLOCKS * N - LATE
 
 FLOPS = 3 * ROWS * N
@@ -46,7 +47,7 @@ def tile_lookup_vg_maxrelu_out_kernel(tc, tab, y, offs, out):
             nc.sync.dma_start(out_rows[b][:, first:last], product[:, first:last])
 
         last_product = held.tile([P, N], F32, name="last_product", align_bytes=ALIGN)
-        late = last_product[:, PIECE - SHORT : 2 * PIECE]
+        late = last_product[:, CUTS[1] - SHORT : CUTS[2]]
         nc.scalar.dma_start(early[:], y_pairs[:, :EARLY])
         nc.sync.dma_start(gates[0][:], gate_rows[0])
         nc.sync.dma_start(offsets[:], offs)
@@ -63,5 +64,5 @@ def tile_lookup_vg_maxrelu_out_kernel(tc, tab, y, offs, out):
 
         look_up_values(1, N - LATE, N - PIECE, late[:, :SHORT])
         look_up_values(1, N - PIECE, N, late[:, SHORT:])
-        for piece in (0, 2, 1, 3):
-            gate_and_store(1, piece * PIECE, (piece + 1) * PIECE, last_product)
+        for first, last in zip(CUTS, CUTS[1:]):
+            gate_and_store(1, first, last, last_product)

@@ -49,8 +49,8 @@ def tile_lookup_vg_maxrelu_out_kernel(tc, tab, y, offs, out):
         last_product = held.tile([P, N], F32, name="last_product", align_bytes=ALIGN)
         late = last_product[:, CUTS[1] - SHORT : CUTS[2]]
         nc.scalar.dma_start(early[:], y_pairs[:, :EARLY])
-        nc.sync.dma_start(gates[0][:], gate_rows[0])
         nc.sync.dma_start(offsets[:], offs)
+        nc.sync.dma_start(gates[0][:], gate_rows[0])
         for b in reversed(range(BLOCKS)):
             nc.sync.dma_start(values[b][:], value_rows[b])
         nc.sync.dma_start(gates[1][:], gate_rows[1])

@@ -14,7 +14,8 @@ PIECE = 128
 SHORT = PIECE // 2
 LATE = SHORT + PIECE
 ALIGN = 256
-CUTS = [0, *range(PIECE + SHORT, N, PIECE), N]
+CUTS = [0, LATE, 2 * LATE, N]
+FIRST_CUTS = [0, SHORT, *range(PIECE, N + 1, PIECE)]
 EARLY = BLOCKS * N - LATE
 
 FLOPS = 3 * ROWS * N
@@ -47,20 +48,20 @@ def tile_lookup_vg_maxrelu_out_kernel(tc, tab, y, offs, out):
             nc.sync.dma_start(out_rows[b][:, first:last], product[:, first:last])
 
         last_product = held.tile([P, N], F32, name="last_product", align_bytes=ALIGN)
-        late = last_product[:, CUTS[1] - SHORT : CUTS[2]]
+        late = last_product[:, CUTS[1] - SHORT : CUTS[1] + PIECE]
         nc.scalar.dma_start(early[:], y_pairs[:, :EARLY])
         nc.sync.dma_start(offsets[:], offs)
         nc.sync.dma_start(gates[0][:], gate_rows[0])
-        for b in reversed(range(BLOCKS)):
+        for b in range(BLOCKS):
             nc.sync.dma_start(values[b][:], value_rows[b])
         nc.sync.dma_start(gates[1][:], gate_rows[1])
         nc.sync.dma_start(late, y_pairs[:, EARLY:])
 
-        look_up_values(1, 0, N - LATE, early[:, N:])
         look_up_values(0, 0, N, early[:, :N])
         product = held.tile([P, N], F32, name="product", align_bytes=ALIGN)
-        for first in range(0, N, PIECE):
-            gate_and_store(0, first, first + PIECE, product)
+        for first, last in zip(FIRST_CUTS, FIRST_CUTS[1:]):
+            gate_and_store(0, first, last, product)
+        look_up_values(1, 0, N - LATE, early[:, N:])
 
         look_up_values(1, N - LATE, N - PIECE, late[:, :SHORT])
         look_up_values(1, N - PIECE, N, late[:, SHORT:])

@@ -12,10 +12,11 @@ BLOCKS = ROWS // P
 STRIPE = 16
 PIECE = 128
 SHORT = PIECE // 2
-LATE = SHORT + PIECE
+LATE = 2 * PIECE
 ALIGN = 256
-CUTS = [0, LATE, 2 * LATE, N]
-FIRST_CUTS = [0, SHORT, *range(PIECE, N + 1, PIECE)]
+CUTS = [0, N - LATE, N - PIECE, N]
+FIRST_CUTS = [*range(0, 2 * PIECE, SHORT), *range(2 * PIECE, N + 1, PIECE)]
+SHARE = 3 * PLACES // 4
 EARLY = BLOCKS * N - LATE
 
 FLOPS = 3 * ROWS * N
@@ -23,13 +24,15 @@ FLOPS = 3 * ROWS * N
 
 def tile_lookup_vg_maxrelu_out_kernel(tc, tab, y, offs, out):
     nc = tc.nc
-    value_rows = tab[0].rearrange("(p b) s -> b p s", b=BLOCKS)
+    value_pairs = tab[0].rearrange("(p b) s -> p (b s)", b=BLOCKS)
     gate_rows = tab[1].rearrange("(p b) s -> b p s", b=BLOCKS)
     y_pairs = y.rearrange("(p b) j -> p (b j)", b=BLOCKS)
     out_rows = out.rearrange("(p b) j -> b p j", b=BLOCKS)
     with tc.tile_pool(name="held", bufs=1) as held:
         offsets = held.tile([P, N // STRIPE], U16, name="offsets", align_bytes=ALIGN)
         early = held.tile([P, EARLY], F32, name="early", align_bytes=ALIGN)
+        both_values = held.tile([P, BLOCKS * PLACES], F32, name="both_values", align_bytes=ALIGN)
+        warm = held.tile([P, 1], F32, name="warm", align_bytes=ALIGN)
         values = [held.tile([P, PLACES], F32, name=f"values{b}", align_bytes=ALIGN) for b in range(BLOCKS)]
         gates = [held.tile([P, PLACES], F32, name=f"gates{b}", align_bytes=ALIGN) for b in range(BLOCKS)]
         top = [held.tile([P, N], F32, name=f"top{b}", align_bytes=ALIGN) for b in range(BLOCKS)]
@@ -48,22 +51,30 @@ def tile_lookup_vg_maxrelu_out_kernel(tc, tab, y, offs, out):
             nc.sync.dma_start(out_rows[b][:, first:last], product[:, first:last])
 
         last_product = held.tile([P, N], F32, name="last_product", align_bytes=ALIGN)
-        late = last_product[:, CUTS[1] - SHORT : CUTS[1] + PIECE]
+        late = last_product[:, CUTS[1] - SHORT : CUTS[1] - SHORT + LATE]
         nc.scalar.dma_start(early[:], y_pairs[:, :EARLY])
         nc.sync.dma_start(offsets[:], offs)
-        nc.sync.dma_start(gates[0][:], gate_rows[0])
+        nc.sync.dma_start(both_values[:], value_pairs)
         for b in range(BLOCKS):
-            nc.sync.dma_start(values[b][:], value_rows[b])
-        nc.sync.dma_start(gates[1][:], gate_rows[1])
+            nc.sync.dma_start(gates[b][:], gate_rows[b])
         nc.sync.dma_start(late, y_pairs[:, EARLY:])
 
+        nc.scalar.activation(warm[:], early[:, :1], RELU, bias=both_values[:, :1])
+        nc.vector.tensor_copy(values[0][:], both_values[:, :PLACES])
+        nc.vector.tensor_copy(values[1][:, :SHARE], both_values[:, PLACES : PLACES + SHARE])
+        nc.scalar.copy(values[1][:, SHARE:], both_values[:, PLACES + SHARE :])
         look_up_values(0, 0, N, early[:, :N])
         product = held.tile([P, N], F32, name="product", align_bytes=ALIGN)
         for first, last in zip(FIRST_CUTS, FIRST_CUTS[1:]):
             gate_and_store(0, first, last, product)
         look_up_values(1, 0, N - LATE, early[:, N:])
 
-        look_up_values(1, N - LATE, N - PIECE, late[:, :SHORT])
-        look_up_values(1, N - PIECE, N, late[:, SHORT:])
-        for first, last in zip(CUTS, CUTS[1:]):
+        def look_up_late(first, last):
+            look_up_values(1, N - LATE + first, N - LATE + last, late[:, first:last])
+
+        look_up_late(0, SHORT)
+        look_up_late(SHORT, SHORT + PIECE)
+        gate_and_store(1, CUTS[0], CUTS[1], last_product)
+        look_up_late(SHORT + PIECE, LATE)
+        for first, last in zip(CUTS[1:], CUTS[2:]):
             gate_and_store(1, first, last, last_product)

@@ -16,7 +16,7 @@ LATE = 2 * PIECE
 ALIGN = 256
 CUTS = [0, N - LATE, N - PIECE, N]
 FIRST_CUTS = [*range(0, 2 * PIECE, SHORT), *range(2 * PIECE, N + 1, PIECE)]
-SHARE = 3 * PLACES // 4
+SHARE = PLACES // 2
 EARLY = BLOCKS * N - LATE
 
 FLOPS = 3 * ROWS * N
@@ -32,6 +32,7 @@ def tile_lookup_vg_maxrelu_out_kernel(tc, tab, y, offs, out):
         offsets = held.tile([P, N // STRIPE], U16, name="offsets", align_bytes=ALIGN)
         early = held.tile([P, EARLY], F32, name="early", align_bytes=ALIGN)
         both_values = held.tile([P, BLOCKS * PLACES], F32, name="both_values", align_bytes=ALIGN)
+        zero = held.tile([P, 1], F32, name="zero", align_bytes=ALIGN)
         warm = held.tile([P, 1], F32, name="warm", align_bytes=ALIGN)
         values = [held.tile([P, PLACES], F32, name=f"values{b}", align_bytes=ALIGN) for b in range(BLOCKS)]
         gates = [held.tile([P, PLACES], F32, name=f"gates{b}", align_bytes=ALIGN) for b in range(BLOCKS)]
@@ -59,7 +60,8 @@ def tile_lookup_vg_maxrelu_out_kernel(tc, tab, y, offs, out):
             nc.sync.dma_start(gates[b][:], gate_rows[b])
         nc.sync.dma_start(late, y_pairs[:, EARLY:])
 
-        nc.scalar.activation(warm[:], early[:, :1], RELU, bias=both_values[:, :1])
+        nc.vector.memset(zero[:], 0.0)
+        nc.scalar.activation(warm[:], early[:, :1], RELU, bias=zero[:])
         nc.vector.tensor_copy(values[0][:], both_values[:, :PLACES])
         nc.vector.tensor_copy(values[1][:, :SHARE], both_values[:, PLACES : PLACES + SHARE])
         nc.scalar.copy(values[1][:, SHARE:], both_values[:, PLACES + SHARE :])

@@ -32,8 +32,6 @@ def tile_lookup_vg_maxrelu_out_kernel(tc, tab, y, offs, out):
         offsets = held.tile([P, N // STRIPE], U16, name="offsets", align_bytes=ALIGN)
         early = held.tile([P, EARLY], F32, name="early", align_bytes=ALIGN)
         both_values = held.tile([P, BLOCKS * PLACES], F32, name="both_values", align_bytes=ALIGN)
-        zero = held.tile([P, 1], F32, name="zero", align_bytes=ALIGN)
-        warm = held.tile([P, 1], F32, name="warm", align_bytes=ALIGN)
         values = [held.tile([P, PLACES], F32, name=f"values{b}", align_bytes=ALIGN) for b in range(BLOCKS)]
         gates = [held.tile([P, PLACES], F32, name=f"gates{b}", align_bytes=ALIGN) for b in range(BLOCKS)]
         top = [held.tile([P, N], F32, name=f"top{b}", align_bytes=ALIGN) for b in range(BLOCKS)]
@@ -60,8 +58,6 @@ def tile_lookup_vg_maxrelu_out_kernel(tc, tab, y, offs, out):
             nc.sync.dma_start(gates[b][:], gate_rows[b])
         nc.sync.dma_start(late, y_pairs[:, EARLY:])
 
-        nc.vector.memset(zero[:], 0.0)
-        nc.scalar.activation(warm[:], early[:, :1], RELU, bias=zero[:])
         nc.vector.tensor_copy(values[0][:], both_values[:, :PLACES])
         nc.vector.tensor_copy(values[1][:, :SHARE], both_values[:, PLACES : PLACES + SHARE])
         nc.scalar.copy(values[1][:, SHARE:], both_values[:, PLACES + SHARE :])

@@ -63,8 +63,12 @@ def tile_lookup_vg_maxrelu_out_kernel(tc, tab, y, offs, out):
         nc.scalar.copy(values[1][:, SHARE:], both_values[:, PLACES + SHARE :])
         look_up_values(0, 0, N, early[:, :N])
         product = held.tile([P, N], F32, name="product", align_bytes=ALIGN)
+        for first in (0, N // 2):
+            half = slice(first, first + N // 2)
+            nc.scalar.activation(gate[0][:, half], gates[0][:].indirect(entries(first, first + N // 2)), RELU)
+            nc.vector.tensor_tensor(product[:, half], top[0][:, half], gate[0][:, half], MULT)
         for first, last in zip(FIRST_CUTS, FIRST_CUTS[1:]):
-            gate_and_store(0, first, last, product)
+            nc.sync.dma_start(out_rows[0][:, first:last], product[:, first:last])
         look_up_values(1, 0, N - LATE, early[:, N:])
 
         def look_up_late(first, last):

@@ -14,8 +14,8 @@ PIECE = 128
 SHORT = PIECE // 2
 LATE = 2 * PIECE
 ALIGN = 256
-CUTS = [0, N - LATE, N - PIECE, N]
-FIRST_CUTS = [*range(0, 2 * PIECE, SHORT), *range(2 * PIECE, N + 1, PIECE)]
+CUTS = [0, PIECE, N - LATE + SHORT, N]
+FIRST_CUTS = [0, SHORT, *range(PIECE, N + 1, PIECE)]
 SHARE = PLACES // 2
 EARLY = BLOCKS * N - LATE
 
@@ -50,13 +50,14 @@ def tile_lookup_vg_maxrelu_out_kernel(tc, tab, y, offs, out):
             nc.sync.dma_start(out_rows[b][:, first:last], product[:, first:last])
 
         last_product = held.tile([P, N], F32, name="last_product", align_bytes=ALIGN)
-        late = last_product[:, CUTS[1] - SHORT : CUTS[1] - SHORT + LATE]
+        late = [last_product[:, start : start + PIECE] for start in (PIECE + SHORT, SHORT)]
         nc.scalar.dma_start(early[:], y_pairs[:, :EARLY])
         nc.sync.dma_start(offsets[:], offs)
         nc.sync.dma_start(both_values[:], value_pairs)
         for b in range(BLOCKS):
             nc.sync.dma_start(gates[b][:], gate_rows[b])
-        nc.sync.dma_start(late, y_pairs[:, EARLY:])
+        for part in range(2):
+            nc.sync.dma_start(late[part], y_pairs[:, EARLY + part * PIECE : EARLY + (part + 1) * PIECE])
 
         nc.vector.tensor_copy(values[0][:], both_values[:, :PLACES])
         nc.vector.tensor_copy(values[1][:, :SHARE], both_values[:, PLACES : PLACES + SHARE])
@@ -71,12 +72,8 @@ def tile_lookup_vg_maxrelu_out_kernel(tc, tab, y, offs, out):
             nc.sync.dma_start(out_rows[0][:, first:last], product[:, first:last])
         look_up_values(1, 0, N - LATE, early[:, N:])
 
-        def look_up_late(first, last):
-            look_up_values(1, N - LATE + first, N - LATE + last, late[:, first:last])
-
-        look_up_late(0, SHORT)
-        look_up_late(SHORT, SHORT + PIECE)
-        gate_and_store(1, CUTS[0], CUTS[1], last_product)
-        look_up_late(SHORT + PIECE, LATE)
-        for first, last in zip(CUTS[1:], CUTS[2:]):
+        look_up_values(1, N - LATE, N - PIECE, late[0])
+        look_up_values(1, N - PIECE, N - SHORT, late[1][:, :SHORT])
+        look_up_values(1, N - SHORT, N, late[1][:, SHORT:])
+        for first, last in zip(CUTS, CUTS[1:]):
             gate_and_store(1, first, last, last_product)

@@ -12,9 +12,9 @@ BLOCKS = ROWS // P
 STRIPE = 16
 PIECE = 128
 SHORT = PIECE // 2
-LATE = 2 * PIECE
+LATE = 2 * PIECE + SHORT
 ALIGN = 256
-CUTS = [0, PIECE, N - LATE + SHORT, N]
+CUTS = [0, PIECE + SHORT, N - PIECE, N]
 FIRST_CUTS = [0, SHORT, *range(PIECE, N + 1, PIECE)]
 SHARE = PLACES // 2
 EARLY = BLOCKS * N - LATE
@@ -50,14 +50,14 @@ def tile_lookup_vg_maxrelu_out_kernel(tc, tab, y, offs, out):
             nc.sync.dma_start(out_rows[b][:, first:last], product[:, first:last])
 
         last_product = held.tile([P, N], F32, name="last_product", align_bytes=ALIGN)
-        late = [last_product[:, start : start + PIECE] for start in (PIECE + SHORT, SHORT)]
+        late = last_product[:, :LATE]
         nc.scalar.dma_start(early[:], y_pairs[:, :EARLY])
         nc.sync.dma_start(offsets[:], offs)
         nc.sync.dma_start(both_values[:], value_pairs)
         for b in range(BLOCKS):
             nc.sync.dma_start(gates[b][:], gate_rows[b])
-        for part in range(2):
-            nc.sync.dma_start(late[part], y_pairs[:, EARLY + part * PIECE : EARLY + (part + 1) * PIECE])
+        for first, last in ((0, PIECE), (PIECE, LATE)):
+            nc.sync.dma_start(late[:, first:last], y_pairs[:, EARLY + first : EARLY + last])
 
         nc.vector.tensor_copy(values[0][:], both_values[:, :PLACES])
         nc.vector.tensor_copy(values[1][:, :SHARE], both_values[:, PLACES : PLACES + SHARE])
@@ -72,8 +72,7 @@ def tile_lookup_vg_maxrelu_out_kernel(tc, tab, y, offs, out):
             nc.sync.dma_start(out_rows[0][:, first:last], product[:, first:last])
         look_up_values(1, 0, N - LATE, early[:, N:])
 
-        look_up_values(1, N - LATE, N - PIECE, late[0])
-        look_up_values(1, N - PIECE, N - SHORT, late[1][:, :SHORT])
-        look_up_values(1, N - SHORT, N, late[1][:, SHORT:])
+        for first, last in ((0, PIECE), (PIECE, PIECE + SHORT), (PIECE + SHORT, LATE)):
+            look_up_values(1, N - LATE + first, N - LATE + last, late[:, first:last])
         for first, last in zip(CUTS, CUTS[1:]):
             gate_and_store(1, first, last, last_product)

@@ -14,7 +14,7 @@ PIECE = 128
 SHORT = PIECE // 2
 LATE = 2 * PIECE + SHORT
 ALIGN = 256
-CUTS = [0, PIECE + SHORT, N - PIECE, N]
+CUTS = [0, 2 * PIECE, N - PIECE, N]
 FIRST_CUTS = [0, SHORT, *range(PIECE, N + 1, PIECE)]
 SHARE = PLACES // 2
 EARLY = BLOCKS * N - LATE
@@ -50,7 +50,7 @@ def tile_lookup_vg_maxrelu_out_kernel(tc, tab, y, offs, out):
             nc.sync.dma_start(out_rows[b][:, first:last], product[:, first:last])
 
         last_product = held.tile([P, N], F32, name="last_product", align_bytes=ALIGN)
-        late = last_product[:, :LATE]
+        late = last_product[:, SHORT : SHORT + LATE]
         nc.scalar.dma_start(early[:], y_pairs[:, :EARLY])
         nc.sync.dma_start(offsets[:], offs)
         nc.sync.dma_start(both_values[:], value_pairs)

@@ -15,8 +15,7 @@ SHORT = PIECE // 2
 LATE = 2 * PIECE + SHORT
 ALIGN = 256
 CUTS = [0, 2 * PIECE, N - PIECE, N]
-FIRST_CUTS = [0, SHORT, *range(PIECE, N + 1, PIECE)]
-SHARE = PLACES // 2
+FIRST_CUTS = [0, PIECE, 2 * PIECE, N]
 EARLY = BLOCKS * N - LATE
 
 FLOPS = 3 * ROWS * N
@@ -24,55 +23,49 @@ FLOPS = 3 * ROWS * N
 
 def tile_lookup_vg_maxrelu_out_kernel(tc, tab, y, offs, out):
     nc = tc.nc
-    value_pairs = tab[0].rearrange("(p b) s -> p (b s)", b=BLOCKS)
+    value_rows = tab[0].rearrange("(p b) s -> b p s", b=BLOCKS)
     gate_rows = tab[1].rearrange("(p b) s -> b p s", b=BLOCKS)
     y_pairs = y.rearrange("(p b) j -> p (b j)", b=BLOCKS)
     out_rows = out.rearrange("(p b) j -> b p j", b=BLOCKS)
     with tc.tile_pool(name="held", bufs=1) as held:
         offsets = held.tile([P, N // STRIPE], U16, name="offsets", align_bytes=ALIGN)
-        early = held.tile([P, EARLY], F32, name="early", align_bytes=ALIGN)
-        both_values = held.tile([P, BLOCKS * PLACES], F32, name="both_values", align_bytes=ALIGN)
+        stream = held.tile([P, EARLY], F32, name="stream", align_bytes=ALIGN)
         values = [held.tile([P, PLACES], F32, name=f"values{b}", align_bytes=ALIGN) for b in range(BLOCKS)]
         gates = [held.tile([P, PLACES], F32, name=f"gates{b}", align_bytes=ALIGN) for b in range(BLOCKS)]
         top = [held.tile([P, N], F32, name=f"top{b}", align_bytes=ALIGN) for b in range(BLOCKS)]
         gate = [held.tile([P, N], F32, name=f"gate{b}", align_bytes=ALIGN) for b in range(BLOCKS)]
+        product = held.tile([P, N], F32, name="product", align_bytes=ALIGN)
 
         def entries(first, last):
             return offsets[:, first // STRIPE : last // STRIPE]
 
-        def look_up_values(b, first, last, stream):
+        def look_up_values(b, first, last, y_part):
             picked = values[b][:].indirect(entries(first, last))
-            nc.vector.tensor_tensor(top[b][:, first:last], picked, stream, MAX)
+            nc.vector.tensor_tensor(top[b][:, first:last], picked, y_part, MAX)
 
-        def gate_and_store(b, first, last, product):
+        def gate_and_multiply(b, first, last, result):
             nc.scalar.activation(gate[b][:, first:last], gates[b][:].indirect(entries(first, last)), RELU)
-            nc.vector.tensor_tensor(product[:, first:last], top[b][:, first:last], gate[b][:, first:last], MULT)
-            nc.sync.dma_start(out_rows[b][:, first:last], product[:, first:last])
+            nc.vector.tensor_tensor(result[:, first:last], top[b][:, first:last], gate[b][:, first:last], MULT)
 
-        last_product = held.tile([P, N], F32, name="last_product", align_bytes=ALIGN)
-        late = last_product[:, SHORT : SHORT + LATE]
-        nc.scalar.dma_start(early[:], y_pairs[:, :EARLY])
         nc.sync.dma_start(offsets[:], offs)
-        nc.sync.dma_start(both_values[:], value_pairs)
-        for b in range(BLOCKS):
-            nc.sync.dma_start(gates[b][:], gate_rows[b])
+        for window, rows in ((gates[0], gate_rows[0]), (values[0], value_rows[0]),
+                             (values[1], value_rows[1]), (gates[1], gate_rows[1])):
+            nc.sync.dma_start(window[:], rows)
+        for first, last in ((0, N // 2), (N // 2, EARLY)):
+            nc.scalar.dma_start(stream[:, first:last], y_pairs[:, first:last])
+
+        look_up_values(0, 0, N, stream[:, :N])
+        late = stream[:, SHORT : SHORT + LATE]
         for first, last in ((0, PIECE), (PIECE, LATE)):
             nc.sync.dma_start(late[:, first:last], y_pairs[:, EARLY + first : EARLY + last])
-
-        nc.vector.tensor_copy(values[0][:], both_values[:, :PLACES])
-        nc.vector.tensor_copy(values[1][:, :SHARE], both_values[:, PLACES : PLACES + SHARE])
-        nc.scalar.copy(values[1][:, SHARE:], both_values[:, PLACES + SHARE :])
-        look_up_values(0, 0, N, early[:, :N])
-        product = held.tile([P, N], F32, name="product", align_bytes=ALIGN)
         for first in (0, N // 2):
-            half = slice(first, first + N // 2)
-            nc.scalar.activation(gate[0][:, half], gates[0][:].indirect(entries(first, first + N // 2)), RELU)
-            nc.vector.tensor_tensor(product[:, half], top[0][:, half], gate[0][:, half], MULT)
+            gate_and_multiply(0, first, first + N // 2, product)
         for first, last in zip(FIRST_CUTS, FIRST_CUTS[1:]):
             nc.sync.dma_start(out_rows[0][:, first:last], product[:, first:last])
-        look_up_values(1, 0, N - LATE, early[:, N:])
+        look_up_values(1, 0, N - LATE, stream[:, N:])
 
         for first, last in ((0, PIECE), (PIECE, PIECE + SHORT), (PIECE + SHORT, LATE)):
             look_up_values(1, N - LATE + first, N - LATE + last, late[:, first:last])
         for first, last in zip(CUTS, CUTS[1:]):
-            gate_and_store(1, first, last, last_product)
+            gate_and_multiply(1, first, last, stream)
+            nc.sync.dma_start(out_rows[1][:, first:last], stream[:, first:last])

@@ -14,8 +14,8 @@ PIECE = 128
 SHORT = PIECE // 2
 LATE = 2 * PIECE + SHORT
 ALIGN = 256
-CUTS = [0, 2 * PIECE, N - PIECE, N]
-FIRST_CUTS = [0, PIECE, 2 * PIECE, N]
+FIRST = N - LATE
+FIRST_CUTS = range(0, N + 1, PIECE)
 EARLY = BLOCKS * N - LATE
 
 FLOPS = 3 * ROWS * N
@@ -45,27 +45,36 @@ def tile_lookup_vg_maxrelu_out_kernel(tc, tab, y, offs, out):
 
         def gate_and_multiply(b, first, last, result):
             nc.scalar.activation(gate[b][:, first:last], gates[b][:].indirect(entries(first, last)), RELU)
-            nc.vector.tensor_tensor(result[:, first:last], top[b][:, first:last], gate[b][:, first:last], MULT)
+            nc.vector.tensor_tensor(result, top[b][:, first:last], gate[b][:, first:last], MULT)
 
         nc.sync.dma_start(offsets[:], offs)
         for window, rows in ((gates[0], gate_rows[0]), (values[0], value_rows[0]),
                              (values[1], value_rows[1]), (gates[1], gate_rows[1])):
             nc.sync.dma_start(window[:], rows)
-        for first, last in ((0, N // 2), (N // 2, EARLY)):
-            nc.scalar.dma_start(stream[:, first:last], y_pairs[:, first:last])
+        nc.scalar.dma_start(stream[:], y_pairs[:, :EARLY])
 
         look_up_values(0, 0, N, stream[:, :N])
-        late = stream[:, SHORT : SHORT + LATE]
+        late = stream[:, :LATE]
         for first, last in ((0, PIECE), (PIECE, LATE)):
             nc.sync.dma_start(late[:, first:last], y_pairs[:, EARLY + first : EARLY + last])
         for first in (0, N // 2):
-            gate_and_multiply(0, first, first + N // 2, product)
+            gate_and_multiply(0, first, first + N // 2, product[:, first : first + N // 2])
         for first, last in zip(FIRST_CUTS, FIRST_CUTS[1:]):
             nc.sync.dma_start(out_rows[0][:, first:last], product[:, first:last])
         look_up_values(1, 0, N - LATE, stream[:, N:])
 
-        for first, last in ((0, PIECE), (PIECE, PIECE + SHORT), (PIECE + SHORT, LATE)):
-            look_up_values(1, N - LATE + first, N - LATE + last, late[:, first:last])
-        for first, last in zip(CUTS, CUTS[1:]):
-            gate_and_multiply(1, first, last, stream)
-            nc.sync.dma_start(out_rows[1][:, first:last], stream[:, first:last])
+        def look_up_late(first, last):
+            look_up_values(1, FIRST + first, FIRST + last, late[:, first:last])
+
+        def finish(first, last, column):
+            result = stream[:, column : column + last - first]
+            gate_and_multiply(1, first, last, result)
+            nc.sync.dma_start(out_rows[1][:, first:last], result)
+
+        look_up_late(0, PIECE)
+        look_up_late(PIECE, PIECE + SHORT)
+        look_up_late(PIECE + SHORT, 2 * PIECE)
+        finish(0, FIRST, 0)
+        look_up_late(2 * PIECE, LATE)
+        finish(FIRST, N - PIECE, LATE)
+        finish(N - PIECE, N, FIRST)

import concourse.mybir as mybir

F32, U16 = mybir.dt.float32, mybir.dt.uint16
MAX, MULT = mybir.AluOpType.max, mybir.AluOpType.mult
RELU = mybir.ActivationFunctionType.Relu

P = 128
ROWS = 256
PLACES = 2048
N = 512
BLOCKS = ROWS // P
STRIPE = 16
PIECE = 128
SHORT = PIECE // 2
LATE = 2 * PIECE + SHORT
ALIGN = 256
FIRST = N - LATE
FIRST_CUTS = range(0, N + 1, PIECE)
EARLY = BLOCKS * N - LATE

FLOPS = 3 * ROWS * N


def tile_lookup_vg_maxrelu_out_kernel(tc, tab, y, offs, out):
    nc = tc.nc
    value_rows = tab[0].rearrange("(p b) s -> b p s", b=BLOCKS)
    gate_rows = tab[1].rearrange("(p b) s -> b p s", b=BLOCKS)
    y_pairs = y.rearrange("(p b) j -> p (b j)", b=BLOCKS)
    out_rows = out.rearrange("(p b) j -> b p j", b=BLOCKS)
    with tc.tile_pool(name="held", bufs=1) as held:
        offsets = held.tile([P, N // STRIPE], U16, name="offsets", align_bytes=ALIGN)
        stream = held.tile([P, EARLY], F32, name="stream", align_bytes=ALIGN)
        values = [held.tile([P, PLACES], F32, name=f"values{b}", align_bytes=ALIGN) for b in range(BLOCKS)]
        gates = [held.tile([P, PLACES], F32, name=f"gates{b}", align_bytes=ALIGN) for b in range(BLOCKS)]
        top = [held.tile([P, N], F32, name=f"top{b}", align_bytes=ALIGN) for b in range(BLOCKS)]
        gate = [held.tile([P, N], F32, name=f"gate{b}", align_bytes=ALIGN) for b in range(BLOCKS)]
        product = held.tile([P, N], F32, name="product", align_bytes=ALIGN)

        def entries(first, last):
            return offsets[:, first // STRIPE : last // STRIPE]

        def look_up_values(b, first, last, y_part):
            picked = values[b][:].indirect(entries(first, last))
            nc.vector.tensor_tensor(top[b][:, first:last], picked, y_part, MAX)

        def gate_and_multiply(b, first, last, result):
            nc.scalar.activation(gate[b][:, first:last], gates[b][:].indirect(entries(first, last)), RELU)
            nc.vector.tensor_tensor(result, top[b][:, first:last], gate[b][:, first:last], MULT)

        nc.sync.dma_start(offsets[:], offs)
        for window, rows in ((gates[0], gate_rows[0]), (values[0], value_rows[0]),
                             (values[1], value_rows[1]), (gates[1], gate_rows[1])):
            nc.sync.dma_start(window[:], rows)
        nc.scalar.dma_start(stream[:], y_pairs[:, :EARLY])

        look_up_values(0, 0, N, stream[:, :N])
        late = stream[:, :LATE]
        for first, last in ((0, PIECE), (PIECE, LATE)):
            nc.sync.dma_start(late[:, first:last], y_pairs[:, EARLY + first : EARLY + last])
        for first in (0, N // 2):
            gate_and_multiply(0, first, first + N // 2, product[:, first : first + N // 2])
        for first, last in zip(FIRST_CUTS, FIRST_CUTS[1:]):
            nc.sync.dma_start(out_rows[0][:, first:last], product[:, first:last])
        look_up_values(1, 0, N - LATE, stream[:, N:])

        def look_up_late(first, last):
            look_up_values(1, FIRST + first, FIRST + last, late[:, first:last])

        def finish(first, last, column):
            result = stream[:, column : column + last - first]
            gate_and_multiply(1, first, last, result)
            nc.sync.dma_start(out_rows[1][:, first:last], result)

        look_up_late(0, PIECE)
        look_up_late(PIECE, PIECE + SHORT)
        look_up_late(PIECE + SHORT, 2 * PIECE)
        finish(0, FIRST, 0)
        look_up_late(2 * PIECE, LATE)
        finish(FIRST, N - PIECE, LATE)
        finish(N - PIECE, N, FIRST)
